import numpy as np, ml_dtypes
CORES = [2,10,50,58,66,74,122]
N = 7
TK = 512
def setup_inputs(rng):
    return {"c": rng.standard_normal((N, 128, 128), dtype=np.float32).astype(ml_dtypes.bfloat16), "x": rng.standard_normal((N, 128, TK), dtype=np.float32).astype(ml_dtypes.bfloat16)}
def setup_inputs_big(rng):
    d = setup_inputs(rng)
    for k in ("c", "x"): d[k] = (d[k].astype(np.float32) * 1024.0).astype(d[k].dtype)
    return d
def setup_inputs_small(rng):
    d = setup_inputs(rng)
    for k in ("c", "x"): d[k] = (d[k].astype(np.float32) * (1 / 1024.0)).astype(d[k].dtype)
    return d
def setup_inputs_apart(rng):
    d = setup_inputs(rng)
    f = (10.0 ** rng.permutation(np.linspace(-1.5, 1.5, N))).astype(np.float32).reshape(N, 1, 1)
    for k in ("c", "x"): d[k] = (d[k].astype(np.float32) * f).astype(d[k].dtype)
    return d
def reference(c, x):
    C, X = c.astype(np.float64), x.astype(np.float64)
    y = np.zeros((N, 128, TK))
    for r in range(N):
        for j in range(N):
            y[r] += C[(r - j) % N].T @ X[j]
    return {"y": y.astype(ml_dtypes.bfloat16 if x.dtype != np.float64 else np.float64)}

@@ -1,0 +1,65 @@
+from concourse.bass import DstId, RemoteDMATransfer
+
+N = 7
+KC = 128
+TK = 512
+W = KC + TK
+
+SCRATCH = {
+    "cx": ("sbuf", [128, W], "bfloat16"),
+    "out": ("sbuf", [128, TK], "bfloat16"),
+    "acc": ("psum", [128, TK], "float32"),
+}
+for _j in range(N):
+    SCRATCH["land%d" % _j] = ("sbuf", [128, W], "bfloat16")
+
+SEMAPHORES = ["ld", "sent", "mm", "cp", "st"] + ["arr%d" % _j for _j in range(N)]
+
+
+def rank_program(g, core, T, topo):
+    r = T.rank_of(core)
+    if r is None:
+        return
+    sem = T.sem
+    cores = T.cores
+
+    g.sync.dma_start(T.cx[:, KC:W], T.x[:]).then_inc(sem.ld, 16)
+    g.scalar.dma_start(T.cx[:, 0:KC], T.c[:]).then_inc(sem.ld, 16)
+
+    dests = [(r + d) % N for d in range(1, N)]
+    mask = topo.mask(core, cores[dests[0]])
+    for d in dests:
+        mask &= topo.mask(core, cores[d])
+    eng = bin(mask).count("1")
+    ids = []
+    for d in dests:
+        rid, pid, _se = topo.addr(cores[d])
+        ids.append(DstId(rid=rid, pnc=pid))
+    g.wait_ge(sem.ld, 32)
+    g.remote_dma_fused(
+        [RemoteDMATransfer(dst_ids=ids, dma_engine_mask=mask, remote_sem=sem["arr%d" % r],
+                           srcs=[T.cx[:]], dsts=[T["land%d" % r][:] for _d in dests], alu_op=0)],
+        local_sem=sem.sent)
+
+    def buf(s):
+        return T.cx if s == r else T["land%d" % s]
+
+    def when(s):
+        return (r - s) % N
+
+    terms = sorted(((j, (r - j) % N) for j in range(N)), key=lambda t: max(when(t[0]), when(t[1])))
+    seen = set()
+    g.tensor.wait_ge(sem.ld, 32)
+    for i, (j, k) in enumerate(terms):
+        for s in (j, k):
+            if s != r and s not in seen:
+                g.tensor.wait_ge(sem["arr%d" % s], eng)
+                seen.add(s)
+        g.tensor.matmul(T.acc[:], buf(k)[:, 0:KC], buf(j)[:, KC:W], i == 0, i == N - 1).then_inc(sem.mm, 1)
+
+    g.vector.wait_ge(sem.mm, N)
+    g.vector.tensor_copy(T.out[:], T.acc[:]).then_inc(sem.cp, 1)
+    g.sync.wait_ge(sem.cp, 1)
+    g.sync.dma_start(T.y[:], T.out[:]).then_inc(sem.st, 16)
+    g.sync.wait_ge(sem.st, 16)
+    g.wait_ge(sem.sent, eng)

@@ -1,65 +1,130 @@
 from concourse.bass import DstId, RemoteDMATransfer
 
 N = 7
+NCORES = 128
 KC = 128
 TK = 512
 W = KC + TK
+HALF = TK // 2
+RELAYED = (6,)
 
 SCRATCH = {
     "cx": ("sbuf", [128, W], "bfloat16"),
     "out": ("sbuf", [128, TK], "bfloat16"),
-    "acc": ("psum", [128, TK], "float32"),
+    "acc0": ("psum", [128, TK], "float32"),
+    "acc1": ("psum", [128, TK], "float32"),
 }
 for _j in range(N):
     SCRATCH["land%d" % _j] = ("sbuf", [128, W], "bfloat16")
 
-SEMAPHORES = ["ld", "sent", "mm", "cp", "st"] + ["arr%d" % _j for _j in range(N)]
+SEMAPHORES = ["ld", "sent", "fed", "mm0", "mm1", "cp0", "cp1", "st"] + ["arr%d" % _j for _j in range(N)]
+
+
+def _relay_of(j, cores, topo):
+    src = cores[j]
+    for h in range(NCORES):
+        if (topo.chip(h) == topo.chip(src) and topo.die(h) != topo.die(src)
+                and all(topo.may_write(h, cores[(j + d) % N]) for d in RELAYED)):
+            return h
+    return None
+
+
+def _ids(dsts, topo):
+    out = []
+    for c in dsts:
+        rid, pid, _se = topo.addr(c)
+        out.append(DstId(rid=rid, pnc=pid))
+    return out
+
+
+def _mask(src, dsts, topo):
+    m = topo.mask(src, dsts[0])
+    for c in dsts:
+        m &= topo.mask(src, c)
+    return m
+
+
+def _count(m):
+    return bin(m).count("1")
 
 
 def rank_program(g, core, T, topo):
-    r = T.rank_of(core)
-    if r is None:
-        return
     sem = T.sem
     cores = T.cores
+    r = T.rank_of(core)
+
+    if r is None:
+        for j in range(N):
+            if _relay_of(j, cores, topo) == core:
+                src = cores[j]
+                far = [cores[(j + d) % N] for d in range(1, N) if d not in RELAYED]
+                fed = _count(topo.mask(src, core) & ~_mask(src, far, topo))
+                dsts = [cores[(j + d) % N] for d in RELAYED]
+                m = _mask(core, dsts, topo)
+                g.wait_ge(sem.fed, fed)
+                g.remote_dma_fused(
+                    [RemoteDMATransfer(dst_ids=_ids(dsts, topo), dma_engine_mask=m, remote_sem=sem["arr%d" % j],
+                                       srcs=[T.cx[:]], dsts=[T["land%d" % j][:] for _d in dsts], alu_op=0)],
+                    local_sem=sem.sent)
+                g.wait_ge(sem.sent, _count(m))
+        return
 
     g.sync.dma_start(T.cx[:, KC:W], T.x[:]).then_inc(sem.ld, 16)
     g.scalar.dma_start(T.cx[:, 0:KC], T.c[:]).then_inc(sem.ld, 16)
 
-    dests = [(r + d) % N for d in range(1, N)]
-    mask = topo.mask(core, cores[dests[0]])
-    for d in dests:
-        mask &= topo.mask(core, cores[d])
-    eng = bin(mask).count("1")
-    ids = []
-    for d in dests:
-        rid, pid, _se = topo.addr(cores[d])
-        ids.append(DstId(rid=rid, pnc=pid))
+    relay = _relay_of(r, cores, topo)
+    far = [cores[(r + d) % N] for d in range(1, N) if d not in RELAYED]
+    m_far = _mask(core, far, topo)
+    m_near = topo.mask(core, relay) & ~m_far
     g.wait_ge(sem.ld, 32)
     g.remote_dma_fused(
-        [RemoteDMATransfer(dst_ids=ids, dma_engine_mask=mask, remote_sem=sem["arr%d" % r],
-                           srcs=[T.cx[:]], dsts=[T["land%d" % r][:] for _d in dests], alu_op=0)],
+        [RemoteDMATransfer(dst_ids=_ids([relay], topo), dma_engine_mask=m_near, remote_sem=sem.fed,
+                           srcs=[T.cx[:]], dsts=[T.cx[:]], alu_op=0),
+         RemoteDMATransfer(dst_ids=_ids(far, topo), dma_engine_mask=m_far, remote_sem=sem["arr%d" % r],
+                           srcs=[T.cx[:]], dsts=[T["land%d" % r][:] for _d in far], alu_op=0)],
         local_sem=sem.sent)
 
     def buf(s):
         return T.cx if s == r else T["land%d" % s]
 
     def when(s):
-        return (r - s) % N
+        d = (r - s) % N
+        return d + N if d in RELAYED else d
+
+    def landed(s):
+        d = (r - s) % N
+        if d in RELAYED:
+            h = _relay_of(s, cores, topo)
+            return _count(_mask(h, [cores[(s + e) % N] for e in RELAYED], topo))
+        return _count(_mask(cores[s], [cores[(s + e) % N] for e in range(1, N) if e not in RELAYED], topo))
 
     terms = sorted(((j, (r - j) % N) for j in range(N)), key=lambda t: max(when(t[0]), when(t[1])))
+    last = max(max(when(j), when(k)) for j, k in terms)
+    early = [t for t in terms if max(when(t[0]), when(t[1])) < last]
+    late = [t for t in terms if max(when(t[0]), when(t[1])) == last]
+    work = [(t, h) for t in early for h in (0, 1)] + [(t, h) for h in (0, 1) for t in late]
+    accs = (T.acc0, T.acc1)
+    mms = (sem.mm0, sem.mm1)
+    done = [0, 0]
     seen = set()
     g.tensor.wait_ge(sem.ld, 32)
-    for i, (j, k) in enumerate(terms):
+    for (j, k), h in work:
         for s in (j, k):
             if s != r and s not in seen:
-                g.tensor.wait_ge(sem["arr%d" % s], eng)
+                g.tensor.wait_ge(sem["arr%d" % s], landed(s))
                 seen.add(s)
-        g.tensor.matmul(T.acc[:], buf(k)[:, 0:KC], buf(j)[:, KC:W], i == 0, i == N - 1).then_inc(sem.mm, 1)
+        lo = KC + h * HALF
+        g.tensor.matmul(accs[h][:, 0:HALF], buf(k)[:, 0:KC], buf(j)[:, lo:lo + HALF],
+                        done[h] == 0, done[h] == N - 1).then_inc(mms[h], 1)
+        done[h] += 1
 
-    g.vector.wait_ge(sem.mm, N)
-    g.vector.tensor_copy(T.out[:], T.acc[:]).then_inc(sem.cp, 1)
-    g.sync.wait_ge(sem.cp, 1)
-    g.sync.dma_start(T.y[:], T.out[:]).then_inc(sem.st, 16)
-    g.sync.wait_ge(sem.st, 16)
-    g.wait_ge(sem.sent, eng)
+    g.vector.wait_ge(sem.mm0, N)
+    g.vector.tensor_copy(T.out[:, 0:HALF], T.acc0[:, 0:HALF]).then_inc(sem.cp0, 1)
+    g.vector.wait_ge(sem.mm1, N)
+    g.vector.tensor_copy(T.out[:, HALF:TK], T.acc1[:, 0:HALF]).then_inc(sem.cp1, 1)
+    g.sync.wait_ge(sem.cp0, 1)
+    g.sync.dma_start(T.y[:, 0:HALF], T.out[:, 0:HALF]).then_inc(sem.st, 16)
+    g.scalar.wait_ge(sem.cp1, 1)
+    g.scalar.dma_start(T.y[:, HALF:TK], T.out[:, HALF:TK]).then_inc(sem.st, 16)
+    g.wait_ge(sem.sent, _count(m_far) + _count(m_near))
+    g.wait_ge(sem.st, 32)

@@ -6,7 +6,8 @@ KC = 128
 TK = 512
 W = KC + TK
 HALF = TK // 2
-RELAYED = (6,)
+RELAYED = (5, 6)
+DIRECT = tuple(d for d in range(1, N) if d not in RELAYED)
 
 SCRATCH = {
     "cx": ("sbuf", [128, W], "bfloat16"),
@@ -17,16 +18,21 @@ SCRATCH = {
 for _j in range(N):
     SCRATCH["land%d" % _j] = ("sbuf", [128, W], "bfloat16")
 
-SEMAPHORES = ["ld", "sent", "fed", "mm0", "mm1", "cp0", "cp1", "st"] + ["arr%d" % _j for _j in range(N)]
+SEMAPHORES = (["ldc", "ldx", "sent", "fedc", "fedx", "mm0", "mm1", "cp0", "cp1", "st"]
+              + ["arr%d" % _j for _j in range(N)]
+              + ["arc%d" % _j for _j in range(N)])
 
 
-def _relay_of(j, cores, topo):
+def _relays_of(j, cores, topo):
     src = cores[j]
-    for h in range(NCORES):
-        if (topo.chip(h) == topo.chip(src) and topo.die(h) != topo.die(src)
-                and all(topo.may_write(h, cores[(j + d) % N]) for d in RELAYED)):
-            return h
-    return None
+    out = {}
+    for d in RELAYED:
+        for h in range(NCORES):
+            if (topo.chip(h) == topo.chip(src) and topo.die(h) != topo.die(src)
+                    and h not in out.values() and topo.may_write(h, cores[(j + d) % N])):
+                out[d] = h
+                break
+    return out
 
 
 def _ids(dsts, topo):
@@ -48,6 +54,20 @@ def _count(m):
     return bin(m).count("1")
 
 
+def _masks_of(j, cores, topo):
+    src = cores[j]
+    m_far = _mask(src, [cores[(j + d) % N] for d in DIRECT], topo)
+    m_near = _mask(src, list(_relays_of(j, cores, topo).values()), topo) & ~m_far
+    return m_far, m_near
+
+
+def _send(g, src_ap, dst_ap, dsts, mask, remote_sem, local_sem, topo):
+    g.remote_dma_fused(
+        [RemoteDMATransfer(dst_ids=_ids(dsts, topo), dma_engine_mask=mask, remote_sem=remote_sem,
+                           srcs=[src_ap], dsts=[dst_ap for _d in dsts], alu_op=0)],
+        local_sem=local_sem)
+
+
 def rank_program(g, core, T, topo):
     sem = T.sem
     cores = T.cores
@@ -55,64 +75,65 @@ def rank_program(g, core, T, topo):
 
     if r is None:
         for j in range(N):
-            if _relay_of(j, cores, topo) == core:
-                src = cores[j]
-                far = [cores[(j + d) % N] for d in range(1, N) if d not in RELAYED]
-                fed = _count(topo.mask(src, core) & ~_mask(src, far, topo))
-                dsts = [cores[(j + d) % N] for d in RELAYED]
-                m = _mask(core, dsts, topo)
-                g.wait_ge(sem.fed, fed)
-                g.remote_dma_fused(
-                    [RemoteDMATransfer(dst_ids=_ids(dsts, topo), dma_engine_mask=m, remote_sem=sem["arr%d" % j],
-                                       srcs=[T.cx[:]], dsts=[T["land%d" % j][:] for _d in dsts], alu_op=0)],
-                    local_sem=sem.sent)
-                g.wait_ge(sem.sent, _count(m))
+            for d, h in _relays_of(j, cores, topo).items():
+                if h != core:
+                    continue
+                fed = _count(_masks_of(j, cores, topo)[1])
+                dst = cores[(j + d) % N]
+                m = topo.mask(core, dst)
+                land = T["land%d" % j]
+                g.wait_ge(sem.fedc, fed)
+                _send(g, T.cx[:, 0:KC], land[:, 0:KC], [dst], m, sem["arc%d" % j], sem.sent, topo)
+                g.wait_ge(sem.fedx, fed)
+                _send(g, T.cx[:, KC:W], land[:, KC:W], [dst], m, sem["arr%d" % j], sem.sent, topo)
+                g.wait_ge(sem.sent, 2 * _count(m))
         return
 
-    g.sync.dma_start(T.cx[:, KC:W], T.x[:]).then_inc(sem.ld, 16)
-    g.scalar.dma_start(T.cx[:, 0:KC], T.c[:]).then_inc(sem.ld, 16)
+    g.scalar.dma_start(T.cx[:, 0:KC], T.c[:]).then_inc(sem.ldc, 16)
+    g.sync.dma_start(T.cx[:, KC:W], T.x[:]).then_inc(sem.ldx, 16)
 
-    relay = _relay_of(r, cores, topo)
-    far = [cores[(r + d) % N] for d in range(1, N) if d not in RELAYED]
-    m_far = _mask(core, far, topo)
-    m_near = topo.mask(core, relay) & ~m_far
-    g.wait_ge(sem.ld, 32)
-    g.remote_dma_fused(
-        [RemoteDMATransfer(dst_ids=_ids([relay], topo), dma_engine_mask=m_near, remote_sem=sem.fed,
-                           srcs=[T.cx[:]], dsts=[T.cx[:]], alu_op=0),
-         RemoteDMATransfer(dst_ids=_ids(far, topo), dma_engine_mask=m_far, remote_sem=sem["arr%d" % r],
-                           srcs=[T.cx[:]], dsts=[T["land%d" % r][:] for _d in far], alu_op=0)],
-        local_sem=sem.sent)
+    relays = list(_relays_of(r, cores, topo).values())
+    far = [cores[(r + d) % N] for d in DIRECT]
+    m_far, m_near = _masks_of(r, cores, topo)
+    g.wait_ge(sem.ldc, 16)
+    _send(g, T.cx[:, 0:KC], T.cx[:, 0:KC], relays, m_near, sem.fedc, sem.sent, topo)
+    g.wait_ge(sem.ldx, 16)
+    _send(g, T.cx[:], T["land%d" % r][:], far, m_far, sem["arr%d" % r], sem.sent, topo)
+    _send(g, T.cx[:, KC:W], T.cx[:, KC:W], relays, m_near, sem.fedx, sem.sent, topo)
 
     def buf(s):
         return T.cx if s == r else T["land%d" % s]
 
-    def when(s):
+    def operand(s, is_c):
         d = (r - s) % N
-        return d + N if d in RELAYED else d
-
-    def landed(s):
-        d = (r - s) % N
+        if d == 0:
+            return 0.0, (sem.ldc if is_c else sem.ldx), 16
         if d in RELAYED:
-            h = _relay_of(s, cores, topo)
-            return _count(_mask(h, [cores[(s + e) % N] for e in RELAYED], topo))
-        return _count(_mask(cores[s], [cores[(s + e) % N] for e in range(1, N) if e not in RELAYED], topo))
+            n = _count(topo.mask(_relays_of(s, cores, topo)[d], core))
+            if is_c:
+                return len(DIRECT) - 0.5, sem["arc%d" % s], n
+            return len(DIRECT) + 0.1 * d, sem["arr%d" % s], n
+        return float(d), sem["arr%d" % s], _count(_masks_of(s, cores, topo)[0])
 
-    terms = sorted(((j, (r - j) % N) for j in range(N)), key=lambda t: max(when(t[0]), when(t[1])))
-    last = max(max(when(j), when(k)) for j, k in terms)
-    early = [t for t in terms if max(when(t[0]), when(t[1])) < last]
-    late = [t for t in terms if max(when(t[0]), when(t[1])) == last]
+    def ready(t):
+        return max(operand(t[0], False)[0], operand(t[1], True)[0])
+
+    terms = sorted(((j, (r - j) % N) for j in range(N)), key=ready)
+    last = ready(terms[-1])
+    early = [t for t in terms if ready(t) < last]
+    late = [t for t in terms if ready(t) == last]
     work = [(t, h) for t in early for h in (0, 1)] + [(t, h) for h in (0, 1) for t in late]
     accs = (T.acc0, T.acc1)
     mms = (sem.mm0, sem.mm1)
     done = [0, 0]
     seen = set()
-    g.tensor.wait_ge(sem.ld, 32)
     for (j, k), h in work:
-        for s in (j, k):
-            if s != r and s not in seen:
-                g.tensor.wait_ge(sem["arr%d" % s], landed(s))
-                seen.add(s)
+        for key in ((j, False), (k, True)):
+            _t, s_, n_ = operand(key[0], key[1])
+            tag = (key[0], key[1] and ((r - key[0]) % N in RELAYED or key[0] == r))
+            if tag not in seen:
+                g.tensor.wait_ge(s_, n_)
+                seen.add(tag)
         lo = KC + h * HALF
         g.tensor.matmul(accs[h][:, 0:HALF], buf(k)[:, 0:KC], buf(j)[:, lo:lo + HALF],
                         done[h] == 0, done[h] == N - 1).then_inc(mms[h], 1)
@@ -126,5 +147,5 @@ def rank_program(g, core, T, topo):
     g.sync.dma_start(T.y[:, 0:HALF], T.out[:, 0:HALF]).then_inc(sem.st, 16)
     g.scalar.wait_ge(sem.cp1, 1)
     g.scalar.dma_start(T.y[:, HALF:TK], T.out[:, HALF:TK]).then_inc(sem.st, 16)
-    g.wait_ge(sem.sent, _count(m_far) + _count(m_near))
+    g.wait_ge(sem.sent, _count(m_far) + 2 * _count(m_near))
     g.wait_ge(sem.st, 32)

@@ -6,8 +6,9 @@ KC = 128
 TK = 512
 W = KC + TK
 HALF = TK // 2
-RELAYED = (5, 6)
-DIRECT = tuple(d for d in range(1, N) if d not in RELAYED)
+DIR_FROM = ((4, 0, 1, 5, 2, 6, 3), (3, 5, 4, 1, 6, 0, 2), (6, 3, 5, 2, 0, 1, 4))
+REL_FROM = ((1, 2, 0, 6, 3, 4, 5), (2, 4, 6, 0, 5, 3, 1), (5, 6, 3, 4, 1, 2, 0))
+NREL = 2
 
 SCRATCH = {
     "cx": ("sbuf", [128, W], "bfloat16"),
@@ -20,19 +21,31 @@ for _j in range(N):
 
 SEMAPHORES = (["ldc", "ldx", "sent", "fedc", "fedx", "mm0", "mm1", "cp0", "cp1", "st"]
               + ["arr%d" % _j for _j in range(N)]
-              + ["arc%d" % _j for _j in range(N)])
+              + ["arc%d" % _j for _j in range(N)]
+              + ["ara%d" % _j for _j in range(N)]
+              + ["arb%d" % _j for _j in range(N)])
+
+
+def _to(table, s):
+    return [rnd.index(s) for rnd in table]
+
+
+def _round(table, s, r):
+    for i, rnd in enumerate(table):
+        if rnd[r] == s:
+            return i
+    return None
 
 
 def _relays_of(j, cores, topo):
     src = cores[j]
-    out = {}
-    for d in RELAYED:
-        for h in range(NCORES):
-            if (topo.chip(h) == topo.chip(src) and topo.die(h) != topo.die(src)
-                    and h not in out.values() and topo.may_write(h, cores[(j + d) % N])):
-                out[d] = h
-                break
-    return out
+    dsts = [cores[q] for q in _to(REL_FROM, j)]
+    out = []
+    for h in range(NCORES):
+        if (topo.chip(h) == topo.chip(src) and topo.die(h) != topo.die(src)
+                and all(topo.may_write(h, c) for c in dsts)):
+            out.append(h)
+    return out[:NREL]
 
 
 def _ids(dsts, topo):
@@ -56,16 +69,21 @@ def _count(m):
 
 def _masks_of(j, cores, topo):
     src = cores[j]
-    m_far = _mask(src, [cores[(j + d) % N] for d in DIRECT], topo)
-    m_near = _mask(src, list(_relays_of(j, cores, topo).values()), topo) & ~m_far
-    return m_far, m_near
+    m_far = _mask(src, [cores[q] for q in _to(DIR_FROM, j)], topo)
+    m_near = _mask(src, _relays_of(j, cores, topo), topo) & ~m_far
+    bits = [b for b in range(m_near.bit_length()) if (m_near >> b) & 1]
+    n = len(bits) // NREL
+    shares = [sum(1 << b for b in bits[h * n:(h + 1) * n]) for h in range(NREL)]
+    return m_far, shares
 
 
-def _send(g, src_ap, dst_ap, dsts, mask, remote_sem, local_sem, topo):
-    g.remote_dma_fused(
-        [RemoteDMATransfer(dst_ids=_ids(dsts, topo), dma_engine_mask=mask, remote_sem=remote_sem,
-                           srcs=[src_ap], dsts=[dst_ap for _d in dsts], alu_op=0)],
-        local_sem=local_sem)
+def _tr(src_ap, dst_ap, dsts, mask, remote_sem, topo):
+    return RemoteDMATransfer(dst_ids=_ids(dsts, topo), dma_engine_mask=mask, remote_sem=remote_sem,
+                             srcs=[src_ap], dsts=[dst_ap for _d in dsts], alu_op=0)
+
+
+def _xcols(h):
+    return KC + h * HALF, KC + (h + 1) * HALF
 
 
 def rank_program(g, core, T, topo):
@@ -75,48 +93,62 @@ def rank_program(g, core, T, topo):
 
     if r is None:
         for j in range(N):
-            for d, h in _relays_of(j, cores, topo).items():
-                if h != core:
-                    continue
-                fed = _count(_masks_of(j, cores, topo)[1])
-                dst = cores[(j + d) % N]
-                m = topo.mask(core, dst)
-                land = T["land%d" % j]
-                g.wait_ge(sem.fedc, fed)
-                _send(g, T.cx[:, 0:KC], land[:, 0:KC], [dst], m, sem["arc%d" % j], sem.sent, topo)
-                g.wait_ge(sem.fedx, fed)
-                _send(g, T.cx[:, KC:W], land[:, KC:W], [dst], m, sem["arr%d" % j], sem.sent, topo)
+            rel = _relays_of(j, cores, topo)
+            if core not in rel:
+                continue
+            h = rel.index(core)
+            shares = _masks_of(j, cores, topo)[1]
+            dsts = [cores[q] for q in _to(REL_FROM, j)]
+            m = _mask(core, dsts, topo)
+            land = T["land%d" % j]
+            arx = sem[("ara%d", "arb%d")[h] % j]
+            lo, hi = _xcols(h)
+            g.wait_ge(sem.fedc, sum(_count(s) for s in shares))
+            g.remote_dma_fused([_tr(T.cx[:, 0:KC], land[:, 0:KC], [dsts[h + 1]], m, sem["arc%d" % j], topo)],
+                               local_sem=sem.sent)
+            g.wait_ge(sem.fedx, _count(shares[h]))
+            if h == 0:
+                g.remote_dma_fused([_tr(T.cx[:, 0:hi], land[:, 0:hi], dsts[0:1], m, arx, topo)], local_sem=sem.sent)
+                g.remote_dma_fused([_tr(T.cx[:, lo:hi], land[:, lo:hi], dsts[1:], m, arx, topo)], local_sem=sem.sent)
+                g.wait_ge(sem.sent, 3 * _count(m))
+            else:
+                g.remote_dma_fused([_tr(T.cx[:, lo:hi], land[:, lo:hi], dsts, m, arx, topo)], local_sem=sem.sent)
                 g.wait_ge(sem.sent, 2 * _count(m))
         return
 
     g.scalar.dma_start(T.cx[:, 0:KC], T.c[:]).then_inc(sem.ldc, 16)
     g.sync.dma_start(T.cx[:, KC:W], T.x[:]).then_inc(sem.ldx, 16)
 
-    relays = list(_relays_of(r, cores, topo).values())
-    far = [cores[(r + d) % N] for d in DIRECT]
-    m_far, m_near = _masks_of(r, cores, topo)
+    relays = _relays_of(r, cores, topo)
+    far = [cores[q] for q in _to(DIR_FROM, r)]
+    m_far, shares = _masks_of(r, cores, topo)
+    m_near = sum(shares)
     g.wait_ge(sem.ldc, 16)
-    _send(g, T.cx[:, 0:KC], T.cx[:, 0:KC], relays, m_near, sem.fedc, sem.sent, topo)
+    g.remote_dma_fused([_tr(T.cx[:, 0:KC], T.cx[:, 0:KC], relays, m_near, sem.fedc, topo)], local_sem=sem.sent)
     g.wait_ge(sem.ldx, 16)
-    _send(g, T.cx[:], T["land%d" % r][:], far, m_far, sem["arr%d" % r], sem.sent, topo)
-    _send(g, T.cx[:, KC:W], T.cx[:, KC:W], relays, m_near, sem.fedx, sem.sent, topo)
+    g.remote_dma_fused([_tr(T.cx[:, _xcols(h)[0]:_xcols(h)[1]], T.cx[:, _xcols(h)[0]:_xcols(h)[1]],
+                            [relays[h]], shares[h], sem.fedx, topo) for h in range(NREL)], local_sem=sem.sent)
+    g.remote_dma_fused([_tr(T.cx[:], T["land%d" % r][:], far, m_far, sem["arr%d" % r], topo)], local_sem=sem.sent)
 
     def buf(s):
         return T.cx if s == r else T["land%d" % s]
 
-    def operand(s, is_c):
-        d = (r - s) % N
-        if d == 0:
-            return 0.0, (sem.ldc if is_c else sem.ldx), 16
-        if d in RELAYED:
-            n = _count(topo.mask(_relays_of(s, cores, topo)[d], core))
+    def operand(s, is_c, h):
+        if s == r:
+            return 0.0, ("ldc" if is_c else "ldx"), 16
+        i = _round(REL_FROM, s, r)
+        if i is not None:
+            rel = _relays_of(s, cores, topo)
+            per = [_count(_mask(q, [cores[e] for e in _to(REL_FROM, s)], topo)) for q in rel]
+            if is_c and i > 0:
+                return 1.5, "arc%d" % s, per[i - 1]
             if is_c:
-                return len(DIRECT) - 0.5, sem["arc%d" % s], n
-            return len(DIRECT) + 0.1 * d, sem["arr%d" % s], n
-        return float(d), sem["arr%d" % s], _count(_masks_of(s, cores, topo)[0])
+                h = 0
+            return 2.3 + 0.4 * i, ("ara%d", "arb%d")[h] % s, per[h]
+        return 1.0 + _round(DIR_FROM, s, r), "arr%d" % s, _count(_masks_of(s, cores, topo)[0])
 
     def ready(t):
-        return max(operand(t[0], False)[0], operand(t[1], True)[0])
+        return max(operand(t[0], False, 0)[0], operand(t[1], True, 0)[0])
 
     terms = sorted(((j, (r - j) % N) for j in range(N)), key=ready)
     last = ready(terms[-1])
@@ -128,14 +160,12 @@ def rank_program(g, core, T, topo):
     done = [0, 0]
     seen = set()
     for (j, k), h in work:
-        for key in ((j, False), (k, True)):
-            _t, s_, n_ = operand(key[0], key[1])
-            tag = (key[0], key[1] and ((r - key[0]) % N in RELAYED or key[0] == r))
-            if tag not in seen:
-                g.tensor.wait_ge(s_, n_)
-                seen.add(tag)
-        lo = KC + h * HALF
-        g.tensor.matmul(accs[h][:, 0:HALF], buf(k)[:, 0:KC], buf(j)[:, lo:lo + HALF],
+        for _t, name, n_ in (operand(j, False, h), operand(k, True, h)):
+            if name not in seen:
+                g.tensor.wait_ge(sem[name], n_)
+                seen.add(name)
+        lo, hi = _xcols(h)
+        g.tensor.matmul(accs[h][:, 0:HALF], buf(k)[:, 0:KC], buf(j)[:, lo:hi],
                         done[h] == 0, done[h] == N - 1).then_inc(mms[h], 1)
         done[h] += 1
 

from concourse.bass import DstId, RemoteDMATransfer

N = 7
NCORES = 128
KC = 128
TK = 512
W = KC + TK
HALF = TK // 2
DIR_FROM = ((4, 0, 1, 5, 2, 6, 3), (3, 5, 4, 1, 6, 0, 2), (6, 3, 5, 2, 0, 1, 4))
REL_FROM = ((1, 2, 0, 6, 3, 4, 5), (2, 4, 6, 0, 5, 3, 1), (5, 6, 3, 4, 1, 2, 0))
NREL = 2

SCRATCH = {
    "cx": ("sbuf", [128, W], "bfloat16"),
    "out": ("sbuf", [128, TK], "bfloat16"),
    "acc0": ("psum", [128, TK], "float32"),
    "acc1": ("psum", [128, TK], "float32"),
}
for _j in range(N):
    SCRATCH["land%d" % _j] = ("sbuf", [128, W], "bfloat16")

SEMAPHORES = (["ldc", "ldx", "sent", "fedc", "fedx", "mm0", "mm1", "cp0", "cp1", "st"]
              + ["arr%d" % _j for _j in range(N)]
              + ["arc%d" % _j for _j in range(N)]
              + ["ara%d" % _j for _j in range(N)]
              + ["arb%d" % _j for _j in range(N)])


def _to(table, s):
    return [rnd.index(s) for rnd in table]


def _round(table, s, r):
    for i, rnd in enumerate(table):
        if rnd[r] == s:
            return i
    return None


def _relays_of(j, cores, topo):
    src = cores[j]
    dsts = [cores[q] for q in _to(REL_FROM, j)]
    out = []
    for h in range(NCORES):
        if (topo.chip(h) == topo.chip(src) and topo.die(h) != topo.die(src)
                and all(topo.may_write(h, c) for c in dsts)):
            out.append(h)
    return out[:NREL]


def _ids(dsts, topo):
    out = []
    for c in dsts:
        rid, pid, _se = topo.addr(c)
        out.append(DstId(rid=rid, pnc=pid))
    return out


def _mask(src, dsts, topo):
    m = topo.mask(src, dsts[0])
    for c in dsts:
        m &= topo.mask(src, c)
    return m


def _count(m):
    return bin(m).count("1")


def _masks_of(j, cores, topo):
    src = cores[j]
    m_far = _mask(src, [cores[q] for q in _to(DIR_FROM, j)], topo)
    m_near = _mask(src, _relays_of(j, cores, topo), topo) & ~m_far
    bits = [b for b in range(m_near.bit_length()) if (m_near >> b) & 1]
    n = len(bits) // NREL
    shares = [sum(1 << b for b in bits[h * n:(h + 1) * n]) for h in range(NREL)]
    return m_far, shares


def _tr(src_ap, dst_ap, dsts, mask, remote_sem, topo):
    return RemoteDMATransfer(dst_ids=_ids(dsts, topo), dma_engine_mask=mask, remote_sem=remote_sem,
                             srcs=[src_ap], dsts=[dst_ap for _d in dsts], alu_op=0)


def _xcols(h):
    return KC + h * HALF, KC + (h + 1) * HALF


def rank_program(g, core, T, topo):
    sem = T.sem
    cores = T.cores
    r = T.rank_of(core)

    if r is None:
        for j in range(N):
            rel = _relays_of(j, cores, topo)
            if core not in rel:
                continue
            h = rel.index(core)
            shares = _masks_of(j, cores, topo)[1]
            dsts = [cores[q] for q in _to(REL_FROM, j)]
            m = _mask(core, dsts, topo)
            land = T["land%d" % j]
            arx = sem[("ara%d", "arb%d")[h] % j]
            lo, hi = _xcols(h)
            g.wait_ge(sem.fedc, sum(_count(s) for s in shares))
            g.remote_dma_fused([_tr(T.cx[:, 0:KC], land[:, 0:KC], [dsts[h + 1]], m, sem["arc%d" % j], topo)],
                               local_sem=sem.sent)
            g.wait_ge(sem.fedx, _count(shares[h]))
            if h == 0:
                g.remote_dma_fused([_tr(T.cx[:, 0:hi], land[:, 0:hi], dsts[0:1], m, arx, topo)], local_sem=sem.sent)
                g.remote_dma_fused([_tr(T.cx[:, lo:hi], land[:, lo:hi], dsts[1:], m, arx, topo)], local_sem=sem.sent)
                g.wait_ge(sem.sent, 3 * _count(m))
            else:
                g.remote_dma_fused([_tr(T.cx[:, lo:hi], land[:, lo:hi], dsts, m, arx, topo)], local_sem=sem.sent)
                g.wait_ge(sem.sent, 2 * _count(m))
        return

    g.scalar.dma_start(T.cx[:, 0:KC], T.c[:]).then_inc(sem.ldc, 16)
    g.sync.dma_start(T.cx[:, KC:W], T.x[:]).then_inc(sem.ldx, 16)

    relays = _relays_of(r, cores, topo)
    far = [cores[q] for q in _to(DIR_FROM, r)]
    m_far, shares = _masks_of(r, cores, topo)
    m_near = sum(shares)
    g.wait_ge(sem.ldc, 16)
    g.remote_dma_fused([_tr(T.cx[:, 0:KC], T.cx[:, 0:KC], relays, m_near, sem.fedc, topo)], local_sem=sem.sent)
    g.wait_ge(sem.ldx, 16)
    g.remote_dma_fused([_tr(T.cx[:, _xcols(h)[0]:_xcols(h)[1]], T.cx[:, _xcols(h)[0]:_xcols(h)[1]],
                            [relays[h]], shares[h], sem.fedx, topo) for h in range(NREL)], local_sem=sem.sent)
    g.remote_dma_fused([_tr(T.cx[:], T["land%d" % r][:], far, m_far, sem["arr%d" % r], topo)], local_sem=sem.sent)

    def buf(s):
        return T.cx if s == r else T["land%d" % s]

    def operand(s, is_c, h):
        if s == r:
            return 0.0, ("ldc" if is_c else "ldx"), 16
        i = _round(REL_FROM, s, r)
        if i is not None:
            rel = _relays_of(s, cores, topo)
            per = [_count(_mask(q, [cores[e] for e in _to(REL_FROM, s)], topo)) for q in rel]
            if is_c and i > 0:
                return 1.5, "arc%d" % s, per[i - 1]
            if is_c:
                h = 0
            return 2.3 + 0.4 * i, ("ara%d", "arb%d")[h] % s, per[h]
        return 1.0 + _round(DIR_FROM, s, r), "arr%d" % s, _count(_masks_of(s, cores, topo)[0])

    def ready(t):
        return max(operand(t[0], False, 0)[0], operand(t[1], True, 0)[0])

    terms = sorted(((j, (r - j) % N) for j in range(N)), key=ready)
    last = ready(terms[-1])
    early = [t for t in terms if ready(t) < last]
    late = [t for t in terms if ready(t) == last]
    work = [(t, h) for t in early for h in (0, 1)] + [(t, h) for h in (0, 1) for t in late]
    accs = (T.acc0, T.acc1)
    mms = (sem.mm0, sem.mm1)
    done = [0, 0]
    seen = set()
    for (j, k), h in work:
        for _t, name, n_ in (operand(j, False, h), operand(k, True, h)):
            if name not in seen:
                g.tensor.wait_ge(sem[name], n_)
                seen.add(name)
        lo, hi = _xcols(h)
        g.tensor.matmul(accs[h][:, 0:HALF], buf(k)[:, 0:KC], buf(j)[:, lo:hi],
                        done[h] == 0, done[h] == N - 1).then_inc(mms[h], 1)
        done[h] += 1

    g.vector.wait_ge(sem.mm0, N)
    g.vector.tensor_copy(T.out[:, 0:HALF], T.acc0[:, 0:HALF]).then_inc(sem.cp0, 1)
    g.vector.wait_ge(sem.mm1, N)
    g.vector.tensor_copy(T.out[:, HALF:TK], T.acc1[:, 0:HALF]).then_inc(sem.cp1, 1)
    g.sync.wait_ge(sem.cp0, 1)
    g.sync.dma_start(T.y[:, 0:HALF], T.out[:, 0:HALF]).then_inc(sem.st, 16)
    g.scalar.wait_ge(sem.cp1, 1)
    g.scalar.dma_start(T.y[:, HALF:TK], T.out[:, HALF:TK]).then_inc(sem.st, 16)
    g.wait_ge(sem.sent, _count(m_far) + 2 * _count(m_near))
    g.wait_ge(sem.st, 32)
